import numpy as np, ml_dtypes
CORES = [10,34,74,98]
N = 4
import mx_ref
BF = ml_dtypes.bfloat16
def rowtile(v, k):
    z = np.concatenate([v, np.zeros((1, v.shape[1]), BF)])
    return np.concatenate([np.ascontiguousarray(z[k[:, 4 * m:4 * m + 4]].transpose(0, 2, 1)).reshape(128, -1) for m in range(k.shape[1] // 4)], axis=1)
def cut(t, i, w=512):
    return t[:, w * i:w * i + w]
def f(rng, *shape):
    return mx_ref.flush((rng.standard_normal(shape, dtype=np.float32) * np.exp2(rng.integers(-2, 3, shape[:-1] + (1,)))).astype(BF))
def wide(rng, *shape, cols=0):
    v = rng.standard_normal(shape, dtype=np.float32) * np.exp2(rng.integers(-12, 13, shape)).astype(np.float32)
    if cols: v *= np.repeat(np.exp2(rng.integers(-cols, cols + 1, shape[:-2] + (1, shape[-1] // 4))) * (rng.random(shape[:-2] + (1, shape[-1] // 4)) > 0.0625), 4, axis=-1).astype(np.float32)
    return mx_ref.flush(v.astype(BF))
T, GW, CAPP = 1024, 512, 256
def counts(rng):
    n = rng.integers(0, CAPP + 1, (N, N))
    for e in range(N):
        if n[:, e].sum() < CAPP: n[rng.integers(0, N), e] = CAPP
    return n
def lists(rng, n):
    l = np.full((N, N, 512), -1)
    for s in range(N):
        for e in range(N): l[s, e, :n[s, e]] = rng.integers(0, T, n[s, e])
    return l
def store(l):
    return np.ascontiguousarray(l.reshape(N, N, 128, 4).transpose(0, 2, 1, 3)).reshape(N, 128, 4 * N).astype(np.int32)
def setup_inputs(rng):
    return {"x": f(rng, N, T, 128), "dy": f(rng, N, T, GW), "pick": store(lists(rng, counts(rng)))}
def setup_inputs_alike(rng):
    d = setup_inputs(rng); l = np.full((N, N, 512), -1); n = rng.integers(CAPP // 2, CAPP + 1)
    l[:, :, :n] = rng.integers(0, T, n)
    d["pick"] = store(l); return d
def setup_inputs_counts(rng):
    d = setup_inputs(rng)
    n = np.array([0, 1, 33, CAPP])[(np.arange(N)[:, None] + np.arange(N) + rng.integers(0, 4)) % 4][rng.permutation(N)]
    d["pick"] = store(lists(rng, n)); return d
def setup_inputs_giant(rng):
    d = setup_inputs(rng); l = lists(rng, rng.integers(64, CAPP + 1, (N, N)))
    for s in range(N):
        k = rng.permutation(T); kx, kg = k[:T // 32], k[T // 32:T // 16]
        d["x"][s, kx] = (d["x"][s, kx].astype(np.float32) * np.float32(4096)).astype(BF)
        d["dy"][s, kg] = (d["dy"][s, kg].astype(np.float32) * np.float32(4096)).astype(BF)
        for e in range(N):
            i = rng.permutation(32)
            l[s, e, i[0]], l[s, e, i[1]] = rng.choice(kx), rng.choice(kg)
    d["pick"] = store(l); return d
def setup_inputs_reversed(rng):
    d = setup_inputs(rng); n = counts(rng); l = lists(rng, n)
    for s in range(N):
        for e in range(N): l[s, e, :n[s, e]] = np.sort(l[s, e, :n[s, e]])[::-1]
    d["pick"] = store(l); return d
def setup_inputs_spread(rng):
    d = setup_inputs(rng); d["x"] = wide(rng, N, T, 128); d["dy"] = wide(rng, N, T, GW)
    d["pick"] = store(lists(rng, rng.integers(CAPP // 2, CAPP + 1, (N, N)))); return d
def check_inputs(d):
    b = []
    for q in ("x", "dy"):
        v = np.abs(np.asarray(d[q]).astype(np.float32))
        if not np.isfinite(v).all() or ((v != 0) & ((v < 2.0 ** -30) | (v > 2.0 ** 30))).any(): b.append(q)
    for s in range(N):
        for e in range(N):
            k = np.asarray(d["pick"][s])[:, 4 * e:4 * e + 4].reshape(-1); n = int((k >= 0).sum())
            if n > CAPP or k.max() >= T or (k[:n] < 0).any() or (k[n:] != -1).any(): b.append("pick")
    return b
def reference(x, dy, pick):
    y = np.zeros((N, 128, GW), np.float32)
    for e in range(N):
        for s in range(N):
            k = pick[s][:, 4 * e:4 * e + 4]
            X, G = mx_ref.quantize(rowtile(x[s], k)), rowtile(dy[s], k)
            for i in range(GW // 512): y[e][:, 512 * i:512 * i + 512] += mx_ref.matmul(X, mx_ref.quantize(cut(G, i, 2048)))
    return {"y": y}

@@ -1,0 +1,163 @@
+from concourse.bass import DstId, RemoteDMATransfer, IndirectOffsetOnAxis
+from concourse.mybir import dt, ActivationFunctionType
+
+PLAN = "d00 tab t01 t10 t11 f0 t20 t21 f1 t30 t31 s2".split()
+
+N = 4
+ROWS = 1024
+XW, GW = 128, 512
+RW = XW + GW
+C = 512
+HALF = GW // 2
+
+SCRATCH = {
+    "idx": ("sbuf", [128, 16], "int32"),
+    "tab": ("dram", [ROWS, RW], "bfloat16"),
+    "ps": ("psum", [128, 1024], "float32"),
+    "yo0": ("sbuf", [128, HALF], "float32"),
+    "yo1": ("sbuf", [128, HALF], "float32"),
+}
+for _k in range(N):
+    SCRATCH["land%d" % _k] = ("sbuf", [128, 2 * RW], "bfloat16")
+    SCRATCH["tile%d" % _k] = ("sbuf", [128, 4 * C], "bfloat16")
+    SCRATCH["cq%d" % _k] = ("sbuf", [128, C], "float8_e4m3fn_x4")
+    SCRATCH["sq%d" % _k] = ("sbuf", [128, C], "uint8")
+for _k in range(N - 1):
+    SCRATCH["cin%d" % _k] = ("sbuf", [128, C], "float8_e4m3fn_x4")
+    SCRATCH["sin%d" % _k] = ("sbuf", [128, C], "uint8")
+
+SEMAPHORES = ["idx", "tab", "tabx", "sent", "mm0", "mm1", "yc0", "yc1", "st0", "st1"]
+for _k in range(N):
+    SEMAPHORES += ["zl%d" % _k, "zt%d" % _k, "cp%d" % _k, "qq%d" % _k, "ga%d_0" % _k, "ga%d_1" % _k]
+for _k in range(N - 1):
+    SEMAPHORES += ["arr%d" % _k]
+
+
+def rank_program(g, core, T, topo):
+    r = T.rank_of(core)
+    if r is None:
+        return
+    cores = T.cores
+    S = T.sem
+    plane = lambda m: sum(1 for a in range(N) if topo.same_plane(topo.chip(cores[a]), topo.chip(cores[a ^ m])))
+    order = sorted(range(1, N), key=lambda m: (plane(m), m))
+    lists = [r ^ m for m in order] + [r]
+    upper, lower = slice(0, 64), slice(64, 128)
+
+    g.sync.dma_start(T.idx[0:64, :], T.pick[0:64, :]).then_inc(S["idx"], 16)
+    g.scalar.dma_start(T.idx[64:128, 0:14], T.pick[0:64, 2:16]).then_inc(S["idx"], 16)
+    g.sync.dma_start(T.tab[:, XW:RW], T.dy[:]).then_inc(S["tab"], 16)
+    g.dma_start(T.tab[:, 0:XW], T.x[:]).then_inc(S["tabx"], 16)
+
+    for k in range(N):
+        g.vector.memset(T["land%d" % k][:], 0.0).then_inc(S["zl%d" % k], 1)
+    for k in range(N):
+        t = T["tile%d" % k]
+        g.vector.memset(t[lower, 0:4 * XW], 0.0).then_inc(S["zt%d" % k], 1)
+        g.vector.memset(t[upper, 4 * (C - XW):4 * C], 0.0).then_inc(S["zt%d" % k], 1)
+
+    def gather(k, i, table):
+        col = 4 * lists[k] + i
+        off = IndirectOffsetOnAxis(ap=T.idx[:, col:col + 1], axis=0)
+        land, sem = T["land%d" % k], S["ga%d_%d" % (k, i)]
+        o = RW * i
+        if table:
+            g.indirect_dma_start(land[:, o:o + RW], None, T.tab[:], off, bounds_check=ROWS - 1, oob_is_err=False).then_inc(sem, 16)
+        else:
+            g.indirect_dma_start(land[:, o + XW:o + RW], None, T.dy[:], off, bounds_check=ROWS - 1, oob_is_err=False).then_inc(sem, 16)
+            g.indirect_dma_start(land[:, o:o + XW], None, T.x[:], off, bounds_check=ROWS - 1, oob_is_err=False).then_inc(sem, 16)
+
+    sent = [0]
+
+    def dest(k):
+        d = cores[lists[k]]
+        rid, pid, _ = topo.addr(d)
+        return d, rid, pid
+
+    def send_fused(k):
+        d, rid, pid = dest(k)
+        es = topo.engines(core, d)
+        per = len(es) // 4
+        groups = [es[per * a:per * (a + 1)] for a in range(4)]
+        last = groups.pop()
+        groups += [last[:per // 2], last[per // 2:]]
+        cq, cin, w = T["cq%d" % k], T["cin%d" % k], C // 4
+        tr = []
+        for a in range(5):
+            if a < 4:
+                src, dst = cq[:, w * a:w * (a + 1)].bitcast(dt.uint8), cin[:, w * a:w * (a + 1)].bitcast(dt.uint8)
+            else:
+                src, dst = T["sq%d" % k][:], T["sin%d" % k][:]
+            tr.append(RemoteDMATransfer(dst_ids=[DstId(rid=rid, pnc=pid)], dma_engine_mask=sum(1 << e for e in groups[a]),
+                                        remote_sem=S["arr%d" % k], src=src, dst=dst))
+        g.remote_dma_fused(tr, local_sem=S["sent"])
+        sent[0] += len(es)
+
+    def send_split(k):
+        d, rid, pid = dest(k)
+        m, n = topo.mask(core, d), len(topo.engines(core, d))
+        g.remote_dma(T["cin%d" % k][:].bitcast(dt.uint8), T["cq%d" % k][:].bitcast(dt.uint8),
+                     S["arr%d" % k], S["sent"], pid, rid, m)
+        g.remote_dma(T["sin%d" % k][:], T["sq%d" % k][:], S["arr%d" % k], S["sent"], pid, rid, m)
+        sent[0] += 2 * n
+
+    def arrivals(k):
+        n = len(topo.engines(cores[lists[k]], core))
+        return n if "f%d" % k in PLAN else 2 * n
+
+    g.wait_ge(S["idx"], 32)
+    for step in PLAN:
+        op, k = step[0], int(step[1]) if step != "tab" else 0
+        if step == "tab":
+            g.wait_ge(S["tabx"], 16)
+            g.wait_ge(S["tab"], 16)
+        elif op in "dt":
+            if step[2] == "0":
+                g.wait_ge(S["zl%d" % k], 1)
+            gather(k, int(step[2]), op == "t")
+        else:
+            g.wait_ge(S["qq%d" % k], 1)
+            send_fused(k) if op == "f" else send_split(k)
+    g.wait_ge(S["sent"], sent[0])
+
+    for k in range(N):
+        land, tile, cp = T["land%d" % k], T["tile%d" % k], S["cp%d" % k]
+        for i in range(2):
+            n = 32 if "d%d%d" % (k, i) in PLAN else 16
+            g.vector.wait_ge(S["ga%d_%d" % (k, i)], n)
+            g.scalar.wait_ge(S["ga%d_%d" % (k, i)], n)
+            o = RW * i
+            for s, p in ((0, upper), (1, lower)):
+                t = i + 2 * s
+                g.vector.tensor_copy(tile[upper, t:4 * (XW + HALF):4], land[p, o:o + XW + HALF]).then_inc(cp, 1)
+                parts = ((tile[lower, 4 * XW + t:4 * (XW + HALF):4], land[p, o + XW + HALF:o + RW]),
+                         (tile[lower, 4 * (XW + HALF) + t:4 * C:4], land[p, o:o + XW]))
+                for a, b in parts:
+                    if s == 0:
+                        g.vector.tensor_copy(a, b).then_inc(cp, 1)
+                    else:
+                        g.scalar.activation(a, b, ActivationFunctionType.Copy).then_inc(cp, 1)
+        g.vector.wait_ge(S["zt%d" % k], 2)
+        g.vector.wait_ge(cp, 12)
+        g.vector.quantize_mx(T["cq%d" % k][:], T["sq%d" % k][:], tile[:]).then_inc(S["qq%d" % k], 1)
+
+    steps = [("cin0", "sin0", "arr0", arrivals(0)), ("cin1", "sin1", "arr1", arrivals(1)), ("cq3", "sq3", "qq3", 1),
+             ("cin2", "sin2", "arr2", arrivals(2))]
+    for j, (c, s, sem, n) in enumerate(steps):
+        g.tensor.wait_ge(S[sem], n)
+        for h, a in ((0, 0), (1, C - XW)):
+            op = g.tensor.matmul_mx(T.ps[:, 512 * h:512 * h + HALF], T[c][:, a:a + XW], T[s][:, a:a + XW],
+                                    T[c][:, XW:XW + HALF], T[s][:, XW:XW + HALF], j == 0, j == len(steps) - 1)
+            if j == len(steps) - 1:
+                op.then_inc(S["mm%d" % h], 1)
+
+    g.vector.wait_ge(S["mm0"], 1)
+    g.vector.tensor_copy(T.yo0[:], T.ps[:, 0:HALF]).then_inc(S["yc0"], 1)
+    g.sync.wait_ge(S["yc0"], 1)
+    g.sync.dma_start(T.y[:, 0:HALF], T.yo0[:]).then_inc(S["st0"], 16)
+    g.sync.wait_ge(S["st0"], 16)
+    g.scalar.wait_ge(S["mm1"], 1)
+    g.scalar.activation(T.yo1[:], T.ps[:, 512:512 + HALF], ActivationFunctionType.Copy).then_inc(S["yc1"], 1)
+    g.scalar.wait_ge(S["yc1"], 1)
+    g.scalar.dma_start(T.y[:, HALF:GW], T.yo1[:]).then_inc(S["st1"], 16)
+    g.scalar.wait_ge(S["st1"], 16)

@@ -1,14 +1,28 @@
 from concourse.bass import DstId, RemoteDMATransfer, IndirectOffsetOnAxis
 from concourse.mybir import dt, ActivationFunctionType
 
-PLAN = "d00 tab t01 t10 t11 f0 t20 t21 f1 t30 t31 s2".split()
-
 N = 4
 ROWS = 1024
 XW, GW = 128, 512
 RW = XW + GW
 C = 512
 HALF = GW // 2
+FRONT = XW + HALF
+CUT = 256
+GX = 128
+
+PLAN = "d00 tab t01 t10 t11 c0 t20 t21 c1 t30 t31 c2 p2".split()
+PRODUCTS = [0, 1, 3, 2]
+
+CALLS = {
+    "c0": ("rank", 0, [("c", 0, C, "far", "all")]),
+    "c1": ("rank", 1, [("c", C, C + CUT, "home", "all"), ("c", C + CUT, 2 * C, "far", (2, 4)), ("p", 0, 2 * C, "far", (3, 4))]),
+    "c2": ("rank", 2, [("c", 2 * C, 3 * C, "home", "all")]),
+    "p2": ("rank", 2, [("p", 2 * C, 3 * C, "home", "all")]),
+    "fc0": ("far", "c0", [("c", 0, C, "home", "all")]),
+    "fc1": ("far", "c1", [("c", C + CUT, 2 * C, "home", "all")]),
+    "fp": ("far", "c1", [("p", 0, C, "home", (0, 2)), ("p", C, 2 * C, "home", (1, 2))]),
+}
 
 SCRATCH = {
     "idx": ("sbuf", [128, 16], "int32"),
@@ -16,38 +30,95 @@ SCRATCH = {
     "ps": ("psum", [128, 1024], "float32"),
     "yo0": ("sbuf", [128, HALF], "float32"),
     "yo1": ("sbuf", [128, HALF], "float32"),
+    "cq": ("sbuf", [128, N * C], "float8_e4m3fn_x4"),
+    "sq": ("sbuf", [128, N * C], "uint8"),
+    "cin": ("sbuf", [128, (N - 1) * C], "float8_e4m3fn_x4"),
+    "sin": ("sbuf", [128, (N - 1) * C], "uint8"),
 }
 for _k in range(N):
     SCRATCH["land%d" % _k] = ("sbuf", [128, 2 * RW], "bfloat16")
     SCRATCH["tile%d" % _k] = ("sbuf", [128, 4 * C], "bfloat16")
-    SCRATCH["cq%d" % _k] = ("sbuf", [128, C], "float8_e4m3fn_x4")
-    SCRATCH["sq%d" % _k] = ("sbuf", [128, C], "uint8")
-for _k in range(N - 1):
-    SCRATCH["cin%d" % _k] = ("sbuf", [128, C], "float8_e4m3fn_x4")
-    SCRATCH["sin%d" % _k] = ("sbuf", [128, C], "uint8")
 
 SEMAPHORES = ["idx", "tab", "tabx", "sent", "mm0", "mm1", "yc0", "yc1", "st0", "st1"]
 for _k in range(N):
-    SEMAPHORES += ["zl%d" % _k, "zt%d" % _k, "cp%d" % _k, "qq%d" % _k, "ga%d_0" % _k, "ga%d_1" % _k]
+    SEMAPHORES += ["zl%d" % _k, "zt%d" % _k, "cp%d" % _k, "cx%d" % _k, "qf%d" % _k, "qq%d" % _k, "ga%d_0" % _k, "ga%d_1" % _k]
 for _k in range(N - 1):
     SEMAPHORES += ["arr%d" % _k]
+SEMAPHORES += ["h" + _s for _s in CALLS]
 
 
 def rank_program(g, core, T, topo):
-    r = T.rank_of(core)
-    if r is None:
-        return
     cores = T.cores
     S = T.sem
     plane = lambda m: sum(1 for a in range(N) if topo.same_plane(topo.chip(cores[a]), topo.chip(cores[a ^ m])))
     order = sorted(range(1, N), key=lambda m: (plane(m), m))
+
+    def team(a):
+        free = [h for h in topo.cores_of(cores[a]) if h != cores[a] and all(topo.may_write(h, c) for c in cores)]
+        return {"rank": cores[a],
+                "far": [h for h in free if topo.die(h) != topo.die(cores[a])][0],
+                "near": [h for h in free if topo.die(h) == topo.die(cores[a])][0]}
+
+    teams = [team(a) for a in range(N)]
+
+    def transfers(a, name):
+        who, _, trs = CALLS[name]
+        src, out = teams[a][who], []
+        for kind, lo, hi, to, share in trs:
+            home = cores[a ^ order[lo // C]]
+            dst = home if to == "home" else teams[a][to]
+            es = topo.engines(src, dst)
+            if share == "rest":
+                es = [e for e in es if e not in topo.engines(src, home)]
+            elif share != "all":
+                es = es[len(es) // share[1] * share[0]:len(es) // share[1] * (share[0] + 1)]
+            out.append((kind, lo, hi, dst, "arr%d" % (lo // C) if to == "home" else "h" + name, es))
+        return out
+
+    def landing(dst, sem):
+        return sum(len(t[5]) for a in range(N) for name in CALLS for t in transfers(a, name) if t[3] == dst and t[4] == sem)
+
+    def view(kind, lo, hi, home):
+        if kind == "c":
+            return T["cin" if home else "cq"][:, lo:hi].bitcast(dt.uint8)
+        return T["sin" if home else "sq"][:, lo:hi]
+
+    def issue(a, name):
+        after = CALLS[name][1]
+        if CALLS[name][0] == "rank":
+            g.wait_ge(S["qf%d" % after], 1)
+            g.wait_ge(S["qq%d" % after], 1)
+        else:
+            g.wait_ge(S["h" + after], landing(core, "h" + after))
+        trs = []
+        for kind, lo, hi, dst, sem, es in transfers(a, name):
+            rid, pid, _ = topo.addr(dst)
+            trs.append((view(kind, lo, hi, dst in cores), view(kind, lo, hi, False), S[sem], pid, rid, sum(1 << e for e in es)))
+        if len(trs) == 1:
+            dst, src, sem, pid, rid, mask = trs[0]
+            g.remote_dma(dst, src, sem, S["sent"], pid, rid, mask)
+        else:
+            g.remote_dma_fused([RemoteDMATransfer(dst_ids=[DstId(rid=rid, pnc=pid)], dma_engine_mask=mask, remote_sem=sem,
+                                                  src=src, dst=dst) for dst, src, sem, pid, rid, mask in trs], local_sem=S["sent"])
+        return sum(len(t[5]) for t in transfers(a, name))
+
+    for a in range(N):
+        for who in ("far", "near"):
+            if teams[a][who] == core:
+                sent = sum([issue(a, name) for name in CALLS if CALLS[name][0] == who])
+                if sent:
+                    g.wait_ge(S["sent"], sent)
+    r = T.rank_of(core)
+    if r is None:
+        return
     lists = [r ^ m for m in order] + [r]
     upper, lower = slice(0, 64), slice(64, 128)
 
     g.sync.dma_start(T.idx[0:64, :], T.pick[0:64, :]).then_inc(S["idx"], 16)
     g.scalar.dma_start(T.idx[64:128, 0:14], T.pick[0:64, 2:16]).then_inc(S["idx"], 16)
     g.sync.dma_start(T.tab[:, XW:RW], T.dy[:]).then_inc(S["tab"], 16)
-    g.dma_start(T.tab[:, 0:XW], T.x[:]).then_inc(S["tabx"], 16)
+    g.scalar.dma_start(T.tab[GX:ROWS, 0:XW], T.x[GX:ROWS, :]).then_inc(S["tab"], 16)
+    g.dma_start(T.tab[0:GX, 0:XW], T.x[0:GX, :]).then_inc(S["tabx"], 16)
 
     for k in range(N):
         g.vector.memset(T["land%d" % k][:], 0.0).then_inc(S["zl%d" % k], 1)
@@ -67,58 +138,19 @@ def rank_program(g, core, T, topo):
             g.indirect_dma_start(land[:, o + XW:o + RW], None, T.dy[:], off, bounds_check=ROWS - 1, oob_is_err=False).then_inc(sem, 16)
             g.indirect_dma_start(land[:, o:o + XW], None, T.x[:], off, bounds_check=ROWS - 1, oob_is_err=False).then_inc(sem, 16)
 
-    sent = [0]
-
-    def dest(k):
-        d = cores[lists[k]]
-        rid, pid, _ = topo.addr(d)
-        return d, rid, pid
-
-    def send_fused(k):
-        d, rid, pid = dest(k)
-        es = topo.engines(core, d)
-        per = len(es) // 4
-        groups = [es[per * a:per * (a + 1)] for a in range(4)]
-        last = groups.pop()
-        groups += [last[:per // 2], last[per // 2:]]
-        cq, cin, w = T["cq%d" % k], T["cin%d" % k], C // 4
-        tr = []
-        for a in range(5):
-            if a < 4:
-                src, dst = cq[:, w * a:w * (a + 1)].bitcast(dt.uint8), cin[:, w * a:w * (a + 1)].bitcast(dt.uint8)
-            else:
-                src, dst = T["sq%d" % k][:], T["sin%d" % k][:]
-            tr.append(RemoteDMATransfer(dst_ids=[DstId(rid=rid, pnc=pid)], dma_engine_mask=sum(1 << e for e in groups[a]),
-                                        remote_sem=S["arr%d" % k], src=src, dst=dst))
-        g.remote_dma_fused(tr, local_sem=S["sent"])
-        sent[0] += len(es)
-
-    def send_split(k):
-        d, rid, pid = dest(k)
-        m, n = topo.mask(core, d), len(topo.engines(core, d))
-        g.remote_dma(T["cin%d" % k][:].bitcast(dt.uint8), T["cq%d" % k][:].bitcast(dt.uint8),
-                     S["arr%d" % k], S["sent"], pid, rid, m)
-        g.remote_dma(T["sin%d" % k][:], T["sq%d" % k][:], S["arr%d" % k], S["sent"], pid, rid, m)
-        sent[0] += 2 * n
-
-    def arrivals(k):
-        n = len(topo.engines(cores[lists[k]], core))
-        return n if "f%d" % k in PLAN else 2 * n
-
+    sent = 0
     g.wait_ge(S["idx"], 32)
     for step in PLAN:
-        op, k = step[0], int(step[1]) if step != "tab" else 0
         if step == "tab":
             g.wait_ge(S["tabx"], 16)
-            g.wait_ge(S["tab"], 16)
-        elif op in "dt":
-            if step[2] == "0":
-                g.wait_ge(S["zl%d" % k], 1)
-            gather(k, int(step[2]), op == "t")
+            g.wait_ge(S["tab"], 32)
+        elif step in CALLS:
+            sent += issue(r, step)
         else:
-            g.wait_ge(S["qq%d" % k], 1)
-            send_fused(k) if op == "f" else send_split(k)
-    g.wait_ge(S["sent"], sent[0])
+            if step[2] == "0":
+                g.wait_ge(S["zl" + step[1]], 1)
+            gather(int(step[1]), int(step[2]), step[0] == "t")
+    g.wait_ge(S["sent"], sent)
 
     for k in range(N):
         land, tile, cp = T["land%d" % k], T["tile%d" % k], S["cp%d" % k]
@@ -127,37 +159,46 @@ def rank_program(g, core, T, topo):
             g.vector.wait_ge(S["ga%d_%d" % (k, i)], n)
             g.scalar.wait_ge(S["ga%d_%d" % (k, i)], n)
             o = RW * i
-            for s, p in ((0, upper), (1, lower)):
-                t = i + 2 * s
-                g.vector.tensor_copy(tile[upper, t:4 * (XW + HALF):4], land[p, o:o + XW + HALF]).then_inc(cp, 1)
-                parts = ((tile[lower, 4 * XW + t:4 * (XW + HALF):4], land[p, o + XW + HALF:o + RW]),
-                         (tile[lower, 4 * (XW + HALF) + t:4 * C:4], land[p, o:o + XW]))
-                for a, b in parts:
-                    if s == 0:
-                        g.vector.tensor_copy(a, b).then_inc(cp, 1)
-                    else:
-                        g.scalar.activation(a, b, ActivationFunctionType.Copy).then_inc(cp, 1)
+            rows = ((i, upper), (i + 2, lower))
+            for t, p in rows:
+                g.vector.tensor_copy(tile[upper, t:4 * FRONT:4], land[p, o:o + FRONT]).then_inc(cp, 1)
+            for t, p in rows:
+                a, b = tile[lower, 4 * XW + t:4 * FRONT:4], land[p, o + FRONT:o + RW]
+                if p == upper:
+                    g.vector.tensor_copy(a, b).then_inc(cp, 1)
+                else:
+                    g.scalar.activation(a, b, ActivationFunctionType.Copy).then_inc(cp, 1)
+            for t, p in rows:
+                g.scalar.activation(tile[lower, 4 * FRONT + t:4 * C:4], land[p, o:o + XW],
+                                    ActivationFunctionType.Copy).then_inc(S["cx%d" % k], 1)
         g.vector.wait_ge(S["zt%d" % k], 2)
-        g.vector.wait_ge(cp, 12)
-        g.vector.quantize_mx(T["cq%d" % k][:], T["sq%d" % k][:], tile[:]).then_inc(S["qq%d" % k], 1)
+        for lo, hi, sem, n in ((0, FRONT, cp, 8), (FRONT, C, S["cx%d" % k], 4)):
+            g.vector.wait_ge(sem, n)
+            g.vector.quantize_mx(T.cq[:, C * k + lo:C * k + hi], T.sq[:, C * k + lo:C * k + hi],
+                                 tile[:, 4 * lo:4 * hi]).then_inc(S["qq%d" % k] if lo else S["qf%d" % k], 1)
 
-    steps = [("cin0", "sin0", "arr0", arrivals(0)), ("cin1", "sin1", "arr1", arrivals(1)), ("cq3", "sq3", "qq3", 1),
-             ("cin2", "sin2", "arr2", arrivals(2))]
-    for j, (c, s, sem, n) in enumerate(steps):
-        g.tensor.wait_ge(S[sem], n)
-        for h, a in ((0, 0), (1, C - XW)):
-            op = g.tensor.matmul_mx(T.ps[:, 512 * h:512 * h + HALF], T[c][:, a:a + XW], T[s][:, a:a + XW],
-                                    T[c][:, XW:XW + HALF], T[s][:, XW:XW + HALF], j == 0, j == len(steps) - 1)
-            if j == len(steps) - 1:
+    for j, k in enumerate(PRODUCTS):
+        if k == N - 1:
+            c, s = T.cq, T.sq
+        else:
+            c, s = T.cin, T.sin
+            g.tensor.wait_ge(S["arr%d" % k], landing(core, "arr%d" % k))
+        moving = slice(C * k + XW, C * k + XW + HALF)
+        for h, a in ((0, C * k), (1, C * k + C - XW)):
+            if k == N - 1:
+                g.tensor.wait_ge(S[("qq%d" if h else "qf%d") % k], 1)
+            op = g.tensor.matmul_mx(T.ps[:, 512 * h:512 * h + HALF], c[:, a:a + XW], s[:, a:a + XW],
+                                    c[:, moving], s[:, moving], j == 0, j == N - 1)
+            if j == N - 1:
                 op.then_inc(S["mm%d" % h], 1)
 
-    g.vector.wait_ge(S["mm0"], 1)
-    g.vector.tensor_copy(T.yo0[:], T.ps[:, 0:HALF]).then_inc(S["yc0"], 1)
-    g.sync.wait_ge(S["yc0"], 1)
-    g.sync.dma_start(T.y[:, 0:HALF], T.yo0[:]).then_inc(S["st0"], 16)
-    g.sync.wait_ge(S["st0"], 16)
-    g.scalar.wait_ge(S["mm1"], 1)
-    g.scalar.activation(T.yo1[:], T.ps[:, 512:512 + HALF], ActivationFunctionType.Copy).then_inc(S["yc1"], 1)
-    g.scalar.wait_ge(S["yc1"], 1)
-    g.scalar.dma_start(T.y[:, HALF:GW], T.yo1[:]).then_inc(S["st1"], 16)
-    g.scalar.wait_ge(S["st1"], 16)
+    g.scalar.wait_ge(S["mm0"], 1)
+    g.scalar.activation(T.yo0[:], T.ps[:, 0:HALF], ActivationFunctionType.Copy).then_inc(S["yc0"], 1)
+    g.scalar.wait_ge(S["yc0"], 1)
+    g.scalar.dma_start(T.y[:, 0:HALF], T.yo0[:]).then_inc(S["st0"], 16)
+    g.scalar.wait_ge(S["st0"], 16)
+    g.vector.wait_ge(S["mm1"], 1)
+    g.vector.tensor_copy(T.yo1[:], T.ps[:, 512:512 + HALF]).then_inc(S["yc1"], 1)
+    g.sync.wait_ge(S["yc1"], 1)
+    g.sync.dma_start(T.y[:, HALF:GW], T.yo1[:]).then_inc(S["st1"], 16)
+    g.sync.wait_ge(S["st1"], 16)

@@ -2,49 +2,65 @@ from concourse.bass import DstId, RemoteDMATransfer, IndirectOffsetOnAxis
 from concourse.mybir import dt, ActivationFunctionType
 
 N = 4
+ALL = 112
 ROWS = 1024
 XW, GW = 128, 512
 RW = XW + GW
 C = 512
-HALF = GW // 2
-FRONT = XW + HALF
-CUT = 256
-GX = 128
+W = 128
+GX = 16
 
-PLAN = "d00 tab t01 t10 t11 c0 t20 t21 c1 t30 t31 c2 p2".split()
-PRODUCTS = [0, 1, 3, 2]
+PLAN = "d00 tab t01 t10 t11 c0 t20 t21 c1 t30 x2 t31 g2 k2".split()
+
+SOURCE = {"u": {"X0": 0, "G0": XW, "G1": XW + W}, "l": {"G0": XW + 2 * W, "G1": XW + 3 * W, "X1": 0}}
+EARLY = ("X0 G0 G1 X1", ["u X0 G0 G1", "l^ G0 G1", "q X0 G0 G1 X1"], ["l_ G0 G1", "l X1"])
+TILES = [
+    EARLY,
+    EARLY,
+    ("X0 X1 G0 G1", ["u X0", "l^ X1", "q X0 X1", "u G0 G1", "q G0 G1"], ["l_ X1", "l G0 G1"]),
+    ("X0 G0 G1 X1", ["u X0 G0", "u G1", "q X0 G0", "q G1", "q X1"], ["l G0", "l G1", "l X1"]),
+]
+PRODUCTS = "000 001 010 011 100 101 110 111 200 210 300 301 310 311 201 211".split()
+COPIES = {"S": ["00", "01"], "V": ["10", "11"]}
+STORES = {"sync": ["00", "10", "11"], "scalar": ["01"]}
 
 CALLS = {
-    "c0": ("rank", 0, [("c", 0, C, "far", "all")]),
-    "c1": ("rank", 1, [("c", C, C + CUT, "home", "all"), ("c", C + CUT, 2 * C, "far", (2, 4)), ("p", 0, 2 * C, "far", (3, 4))]),
-    "c2": ("rank", 2, [("c", 2 * C, 3 * C, "home", "all")]),
-    "p2": ("rank", 2, [("p", 2 * C, 3 * C, "home", "all")]),
-    "fc0": ("far", "c0", [("c", 0, C, "home", "all")]),
-    "fc1": ("far", "c1", [("c", C + CUT, 2 * C, "home", "all")]),
-    "fp": ("far", "c1", [("p", 0, C, "home", (0, 2)), ("p", C, 2 * C, "home", (1, 2))]),
+    "c0": ("rank", ["q0_0"], [("c", 0, 256, "near", (8, 16, 4)), ("c", 256, 512, "far", (10, 16, 4))]),
+    "c1": ("rank", ["q1_0"], [("c", 512, 768, "home", (0, 8, 2)), ("c", 768, 1024, "far", (8, 16, 2)), ("p", 0, 1024, "near", (1, 8, 2))]),
+    "x2": ("rank", ["q2_0"], [("c", 1024, 1152, "home", (0, 8, 1)), ("c", 1152, 1280, "far", (8, 16, 2))]),
+    "g2": ("rank", ["q2_1"], [("c", 1280, 1408, "home", (0, 8, 2)), ("p", 1024, 1536, "home", (1, 8, 2))]),
+    "k2": ("rank", ["q2_1"], [("c", 1408, 1536, "home", (0, 8, 1))]),
+    "n0": ("near", ["hc0"], [("c", 0, 256, "door", (0, 8, 1))]),
+    "f0": ("far", ["hc0"], [("c", 256, 512, "home", (0, 8, 1))]),
+    "f1": ("far", ["hc1"], [("c", 768, 1024, "home", (0, 8, 1))]),
+    "n1": ("near", ["hc1"], [("p", 0, 512, "home", (0, 4, 1)), ("p", 512, 1024, "home", (4, 8, 1))]),
+    "f2": ("far", ["hx2"], [("c", 1152, 1280, "home", (0, 8, 1))]),
+    "d0": ("door", ["hn0"], [("c", 0, 256, "home", (0, 8, 1))]),
 }
 
 SCRATCH = {
     "idx": ("sbuf", [128, 16], "int32"),
     "tab": ("dram", [ROWS, RW], "bfloat16"),
-    "ps": ("psum", [128, 1024], "float32"),
-    "yo0": ("sbuf", [128, HALF], "float32"),
-    "yo1": ("sbuf", [128, HALF], "float32"),
+    "ps": ("psum", [128, 2048], "float32"),
+    "yo": ("sbuf", [128, GW], "float32"),
     "cq": ("sbuf", [128, N * C], "float8_e4m3fn_x4"),
     "sq": ("sbuf", [128, N * C], "uint8"),
     "cin": ("sbuf", [128, (N - 1) * C], "float8_e4m3fn_x4"),
     "sin": ("sbuf", [128, (N - 1) * C], "uint8"),
+    "land": ("sbuf", [128, 2 * N * RW], "bfloat16"),
 }
 for _k in range(N):
-    SCRATCH["land%d" % _k] = ("sbuf", [128, 2 * RW], "bfloat16")
     SCRATCH["tile%d" % _k] = ("sbuf", [128, 4 * C], "bfloat16")
 
-SEMAPHORES = ["idx", "tab", "tabx", "sent", "mm0", "mm1", "yc0", "yc1", "st0", "st1"]
+SEMAPHORES = ["idx", "tab", "tabx", "sent", "stsync", "stscalar"]
+for _q in ("00", "01", "10", "11"):
+    SEMAPHORES += ["mm" + _q, "yc" + _q]
 for _k in range(N):
-    SEMAPHORES += ["zl%d" % _k, "zt%d" % _k, "cp%d" % _k, "cx%d" % _k, "qf%d" % _k, "qq%d" % _k, "ga%d_0" % _k, "ga%d_1" % _k]
-for _k in range(N - 1):
-    SEMAPHORES += ["arr%d" % _k]
-SEMAPHORES += ["h" + _s for _s in CALLS]
+    SEMAPHORES += ["zt%d" % _k, "ga%d_0" % _k, "ga%d_1" % _k]
+    for _j in range(4):
+        SEMAPHORES += ["cp%d_%d" % (_k, _j), "q%d_%d" % (_k, _j)]
+for _s in CALLS:
+    SEMAPHORES += ["h" + _s] + sorted(set("a%s_%d" % (_s, _t[1] // C) for _t in CALLS[_s][2] if _t[3] == "home"))
 
 
 def rank_program(g, core, T, topo):
@@ -54,25 +70,31 @@ def rank_program(g, core, T, topo):
     order = sorted(range(1, N), key=lambda m: (plane(m), m))
 
     def team(a):
-        free = [h for h in topo.cores_of(cores[a]) if h != cores[a] and all(topo.may_write(h, c) for c in cores)]
-        return {"rank": cores[a],
-                "far": [h for h in free if topo.die(h) != topo.die(cores[a])][0],
-                "near": [h for h in free if topo.die(h) == topo.die(cores[a])][0]}
+        c = cores[a]
+        free = [h for h in topo.cores_of(c) if h != c and all(topo.may_write(h, d) for d in cores)]
+        doors = [h for h in range(ALL) if topo.mates(topo.chip(h), topo.chip(c)) and topo.may_write(h, c)]
+        far = [h for h in free if topo.die(h) != topo.die(c)]
+        return {"rank": c, "far": far[0], "far2": far[1],
+                "near": [h for h in free if topo.die(h) == topo.die(c)][0],
+                "door": [h for h in doors if topo.die(h) == topo.die(c)][0],
+                "door2": [h for h in doors if topo.die(h) != topo.die(c)][0]}
 
     teams = [team(a) for a in range(N)]
 
+    def role(a, who, col):
+        home = a ^ order[col // C]
+        if who == "home":
+            return cores[home]
+        return teams[home if who.startswith("door") else a][who]
+
+    issuer = lambda a, name: role(a, CALLS[name][0], CALLS[name][2][0][1])
+
     def transfers(a, name):
-        who, _, trs = CALLS[name]
-        src, out = teams[a][who], []
-        for kind, lo, hi, to, share in trs:
-            home = cores[a ^ order[lo // C]]
-            dst = home if to == "home" else teams[a][to]
-            es = topo.engines(src, dst)
-            if share == "rest":
-                es = [e for e in es if e not in topo.engines(src, home)]
-            elif share != "all":
-                es = es[len(es) // share[1] * share[0]:len(es) // share[1] * (share[0] + 1)]
-            out.append((kind, lo, hi, dst, "arr%d" % (lo // C) if to == "home" else "h" + name, es))
+        src, out = issuer(a, name), []
+        for kind, lo, hi, to, share in CALLS[name][2]:
+            dst = role(a, to, lo)
+            out.append((kind, lo, hi, dst, "a%s_%d" % (name, lo // C) if to == "home" else "h" + name,
+                        topo.engines(src, dst)[slice(*share)]))
         return out
 
     def landing(dst, sem):
@@ -83,13 +105,16 @@ def rank_program(g, core, T, topo):
             return T["cin" if home else "cq"][:, lo:hi].bitcast(dt.uint8)
         return T["sin" if home else "sq"][:, lo:hi]
 
+    waited = []
+
+    def wait(q, sem):
+        if (q, sem) not in waited:
+            waited.append((q, sem))
+            (g.tensor if q == "tensor" else g).wait_ge(S[sem], 1 if sem[0] == "q" else 16 if sem[0] == "g" else landing(core, sem))
+
     def issue(a, name):
-        after = CALLS[name][1]
-        if CALLS[name][0] == "rank":
-            g.wait_ge(S["qf%d" % after], 1)
-            g.wait_ge(S["qq%d" % after], 1)
-        else:
-            g.wait_ge(S["h" + after], landing(core, "h" + after))
+        for sem in CALLS[name][1]:
+            wait("g", sem)
         trs = []
         for kind, lo, hi, dst, sem, es in transfers(a, name):
             rid, pid, _ = topo.addr(dst)
@@ -102,103 +127,113 @@ def rank_program(g, core, T, topo):
                                                   src=src, dst=dst) for dst, src, sem, pid, rid, mask in trs], local_sem=S["sent"])
         return sum(len(t[5]) for t in transfers(a, name))
 
-    for a in range(N):
-        for who in ("far", "near"):
-            if teams[a][who] == core:
-                sent = sum([issue(a, name) for name in CALLS if CALLS[name][0] == who])
-                if sent:
-                    g.wait_ge(S["sent"], sent)
     r = T.rank_of(core)
     if r is None:
+        sent = sum([issue(a, name) for name in CALLS for a in range(N) if issuer(a, name) == core])
+        if sent:
+            g.wait_ge(S["sent"], sent)
         return
     lists = [r ^ m for m in order] + [r]
-    upper, lower = slice(0, 64), slice(64, 128)
+    half = {"u": slice(0, 64), "l": slice(64, 128)}
 
     g.sync.dma_start(T.idx[0:64, :], T.pick[0:64, :]).then_inc(S["idx"], 16)
     g.scalar.dma_start(T.idx[64:128, 0:14], T.pick[0:64, 2:16]).then_inc(S["idx"], 16)
     g.sync.dma_start(T.tab[:, XW:RW], T.dy[:]).then_inc(S["tab"], 16)
     g.scalar.dma_start(T.tab[GX:ROWS, 0:XW], T.x[GX:ROWS, :]).then_inc(S["tab"], 16)
     g.dma_start(T.tab[0:GX, 0:XW], T.x[0:GX, :]).then_inc(S["tabx"], 16)
+    g.sync.wait_ge(S["tabx"], 16)
+    g.sync.sem_inc(S["tab"], 1)
 
+    column = lambda k, part: W * TILES[k][0].split().index(part)
+    g.vector.memset(T.land[:, 0:RW], 0.0).then_inc(S["idx"], 1)
+    g.vector.memset(T.land[:, RW:2 * N * RW], 0.0).then_inc(S["tab"], 1)
     for k in range(N):
-        g.vector.memset(T["land%d" % k][:], 0.0).then_inc(S["zl%d" % k], 1)
-    for k in range(N):
-        t = T["tile%d" % k]
-        g.vector.memset(t[lower, 0:4 * XW], 0.0).then_inc(S["zt%d" % k], 1)
-        g.vector.memset(t[upper, 4 * (C - XW):4 * C], 0.0).then_inc(S["zt%d" % k], 1)
+        for h, part in (("l", "X0"), ("u", "X1")):
+            c = column(k, part)
+            g.vector.memset(T["tile%d" % k][half[h], 4 * c:4 * (c + W)], 0.0).then_inc(S["zt%d" % k], 1)
 
     def gather(k, i, table):
         col = 4 * lists[k] + i
         off = IndirectOffsetOnAxis(ap=T.idx[:, col:col + 1], axis=0)
-        land, sem = T["land%d" % k], S["ga%d_%d" % (k, i)]
-        o = RW * i
-        if table:
-            g.indirect_dma_start(land[:, o:o + RW], None, T.tab[:], off, bounds_check=ROWS - 1, oob_is_err=False).then_inc(sem, 16)
-        else:
-            g.indirect_dma_start(land[:, o + XW:o + RW], None, T.dy[:], off, bounds_check=ROWS - 1, oob_is_err=False).then_inc(sem, 16)
-            g.indirect_dma_start(land[:, o:o + XW], None, T.x[:], off, bounds_check=ROWS - 1, oob_is_err=False).then_inc(sem, 16)
+        sem = S["ga%d_%d" % (k, i)]
+        o = RW * (2 * k + i)
+        for lo, hi, src in [(0, RW, T.tab)] if table else [(XW, RW, T.dy), (0, XW, T.x)]:
+            g.indirect_dma_start(T.land[:, o + lo:o + hi], None, src[:], off, bounds_check=ROWS - 1, oob_is_err=False).then_inc(sem, 16)
 
     sent = 0
-    g.wait_ge(S["idx"], 32)
+    g.wait_ge(S["idx"], 33)
     for step in PLAN:
         if step == "tab":
-            g.wait_ge(S["tabx"], 16)
-            g.wait_ge(S["tab"], 32)
+            g.wait_ge(S["tab"], 34)
         elif step in CALLS:
             sent += issue(r, step)
         else:
-            if step[2] == "0":
-                g.wait_ge(S["zl" + step[1]], 1)
             gather(int(step[1]), int(step[2]), step[0] == "t")
     g.wait_ge(S["sent"], sent)
 
+    group = {}
     for k in range(N):
-        land, tile, cp = T["land%d" % k], T["tile%d" % k], S["cp%d" % k]
+        tile = T["tile%d" % k]
+        calls = [w.split()[1:] for w in TILES[k][1] if w[0] == "q"]
+        for j, parts in enumerate(calls):
+            for part in parts:
+                group[k, part] = j
+        first = lambda parts: min(group[k, part] for part in parts)
+        sources = lambda op: [("u", 0), ("l", 2)][op[1:] == "_":2 - (op[1:] == "^")]
+        copies = [w.split() for w in TILES[k][1] + TILES[k][2] if w[0] != "q"]
+        count = [2 * sum(len(sources(w[0])) for w in copies if first(w[1:]) == j) for j in range(len(calls))]
         for i in range(2):
-            n = 32 if "d%d%d" % (k, i) in PLAN else 16
-            g.vector.wait_ge(S["ga%d_%d" % (k, i)], n)
-            g.scalar.wait_ge(S["ga%d_%d" % (k, i)], n)
-            o = RW * i
-            rows = ((i, upper), (i + 2, lower))
-            for t, p in rows:
-                g.vector.tensor_copy(tile[upper, t:4 * FRONT:4], land[p, o:o + FRONT]).then_inc(cp, 1)
-            for t, p in rows:
-                a, b = tile[lower, 4 * XW + t:4 * FRONT:4], land[p, o + FRONT:o + RW]
-                if p == upper:
-                    g.vector.tensor_copy(a, b).then_inc(cp, 1)
-                else:
-                    g.scalar.activation(a, b, ActivationFunctionType.Copy).then_inc(cp, 1)
-            for t, p in rows:
-                g.scalar.activation(tile[lower, 4 * FRONT + t:4 * C:4], land[p, o:o + XW],
-                                    ActivationFunctionType.Copy).then_inc(S["cx%d" % k], 1)
-        g.vector.wait_ge(S["zt%d" % k], 2)
-        for lo, hi, sem, n in ((0, FRONT, cp, 8), (FRONT, C, S["cx%d" % k], 4)):
-            g.vector.wait_ge(sem, n)
-            g.vector.quantize_mx(T.cq[:, C * k + lo:C * k + hi], T.sq[:, C * k + lo:C * k + hi],
-                                 tile[:, 4 * lo:4 * hi]).then_inc(S["qq%d" % k] if lo else S["qf%d" % k], 1)
+            o = RW * (2 * k + i)
+            for q, work in ((g.vector, TILES[k][1]), (g.scalar, TILES[k][2])):
+                q.wait_ge(S["ga%d_%d" % (k, i)], 32 if "d%d%d" % (k, i) in PLAN else 16)
+                for op, *parts in [w.split() for w in work]:
+                    lo, n = column(k, parts[0]), W * len(parts)
+                    if op != "q":
+                        for p, t in sources(op):
+                            a = tile[half[op[0]], 4 * lo + i + t:4 * (lo + n):4]
+                            s = o + SOURCE[op[0]][parts[0]]
+                            b = T.land[half[p], s:s + n]
+                            call = q.tensor_copy(a, b) if work is TILES[k][1] else q.activation(a, b, ActivationFunctionType.Copy)
+                            call.then_inc(S["cp%d_%d" % (k, first(parts))], 1)
+                    elif i == 1:
+                        j = first(parts)
+                        if j == 0:
+                            q.wait_ge(S["zt%d" % k], 2)
+                        if count[j]:
+                            q.wait_ge(S["cp%d_%d" % (k, j)], count[j])
+                        c = slice(C * k + lo, C * k + lo + n)
+                        q.quantize_mx(T.cq[:, c], T.sq[:, c], tile[:, 4 * lo:4 * (lo + n)]).then_inc(S["q%d_%d" % (k, j)], 1)
 
-    for j, k in enumerate(PRODUCTS):
-        if k == N - 1:
-            c, s = T.cq, T.sq
-        else:
-            c, s = T.cin, T.sin
-            g.tensor.wait_ge(S["arr%d" % k], landing(core, "arr%d" % k))
-        moving = slice(C * k + XW, C * k + XW + HALF)
-        for h, a in ((0, C * k), (1, C * k + C - XW)):
+    bank = lambda q: T.ps[:, 512 * int(q, 2):512 * int(q, 2) + W]
+    for j, step in enumerate(PRODUCTS):
+        k, q = int(step[0]), step[1:]
+        sides = []
+        for part in ("X" + q[0], "G" + q[1]):
+            lo = C * k + column(k, part)
             if k == N - 1:
-                g.tensor.wait_ge(S[("qq%d" if h else "qf%d") % k], 1)
-            op = g.tensor.matmul_mx(T.ps[:, 512 * h:512 * h + HALF], c[:, a:a + XW], s[:, a:a + XW],
-                                    c[:, moving], s[:, moving], j == 0, j == N - 1)
-            if j == N - 1:
-                op.then_inc(S["mm%d" % h], 1)
+                wait("tensor", "q%d_%d" % (k, group[k, part]))
+            else:
+                for a in range(N):
+                    for name in CALLS:
+                        for t in transfers(a, name):
+                            if t[3] == core and t[1] < lo + W and lo < t[2]:
+                                wait("tensor", t[4])
+            sides += [T["cq" if k == N - 1 else "cin"][:, lo:lo + W], T["sq" if k == N - 1 else "sin"][:, lo:lo + W]]
+        mine = [s for s in PRODUCTS if s[1:] == q]
+        op = g.tensor.matmul_mx(bank(q), *sides, step == mine[0], step == mine[-1])
+        if step == mine[-1]:
+            op.then_inc(S["mm" + q], 1)
 
-    g.scalar.wait_ge(S["mm0"], 1)
-    g.scalar.activation(T.yo0[:], T.ps[:, 0:HALF], ActivationFunctionType.Copy).then_inc(S["yc0"], 1)
-    g.scalar.wait_ge(S["yc0"], 1)
-    g.scalar.dma_start(T.y[:, 0:HALF], T.yo0[:]).then_inc(S["st0"], 16)
-    g.scalar.wait_ge(S["st0"], 16)
-    g.vector.wait_ge(S["mm1"], 1)
-    g.vector.tensor_copy(T.yo1[:], T.ps[:, 512:512 + HALF]).then_inc(S["yc1"], 1)
-    g.sync.wait_ge(S["yc1"], 1)
-    g.sync.dma_start(T.y[:, HALF:GW], T.yo1[:]).then_inc(S["st1"], 16)
-    g.sync.wait_ge(S["st1"], 16)
+    cols = lambda qs: slice(W * int(qs[0], 2), W * int(qs[-1], 2) + W)
+    for q in COPIES["S"]:
+        g.scalar.wait_ge(S["mm" + q], 1)
+        g.scalar.activation(T.yo[:, cols([q])], bank(q), ActivationFunctionType.Copy).then_inc(S["yc" + q], 1)
+    for q in COPIES["V"]:
+        g.vector.wait_ge(S["mm" + q], 1)
+        g.vector.tensor_copy(T.yo[:, cols([q])], bank(q)).then_inc(S["yc" + q], 1)
+    for name, queue in (("sync", g.sync), ("scalar", g.scalar)):
+        for qs in STORES[name]:
+            for q in qs.split():
+                queue.wait_ge(S["yc" + q], 1)
+            queue.dma_start(T.y[:, cols(qs.split())], T.yo[:, cols(qs.split())]).then_inc(S["st" + name], 16)
+        queue.wait_ge(S["st" + name], 16 * len(STORES[name]))

@@ -1,63 +1,91 @@
 from concourse.bass import DstId, RemoteDMATransfer, IndirectOffsetOnAxis
-from concourse.mybir import dt, ActivationFunctionType
+from concourse.mybir import dt, ActivationFunctionType, AluOpType
 
 N = 4
 ALL = 112
 ROWS = 1024
 XW, GW = 128, 512
-RW = XW + GW
 C = 512
 W = 128
-GX = 16
+GRP = 16
+F = XW // GRP
+XP = 64
+R = 2
+PK = 2 * 256 * F // R
 
-PLAN = "d00 tab t01 t10 t11 c0 t20 t21 c1 t30 x2 t31 g2 k2".split()
+PLAN = "d00 d01 z1 d10 d11 c0 d20 b1 d21 c1 d30 x2 d31 g2 k2".split()
 
-SOURCE = {"u": {"X0": 0, "G0": XW, "G1": XW + W}, "l": {"G0": XW + 2 * W, "G1": XW + 3 * W, "X1": 0}}
-EARLY = ("X0 G0 G1 X1", ["u X0 G0 G1", "l^ G0 G1", "q X0 G0 G1 X1"], ["l_ G0 G1", "l X1"])
-TILES = [
-    EARLY,
-    EARLY,
-    ("X0 X1 G0 G1", ["u X0", "l^ X1", "q X0 X1", "u G0 G1", "q G0 G1"], ["l_ X1", "l G0 G1"]),
-    ("X0 G0 G1 X1", ["u X0 G0", "u G1", "q X0 G0", "q G1", "q X1"], ["l G0", "l G1", "l X1"]),
-]
-PRODUCTS = "000 001 010 011 100 101 110 111 200 210 300 301 310 311 201 211".split()
+TILES = ["G0 G1|X0 X1", "X0 X1|G0 G1", "G0 G1|X0 X1", "X0 X1|G0|G1"]
+SOURCE = {"u": {"G0": 0, "G1": W}, "l": {"G0": 2 * W, "G1": 3 * W}}
+VECTOR = ["z 0 2 idx", "zb", "z 2 4 z1", "small", "turn 0 2", "turn 2 6", "turn 6 10", "offsets",
+          "g 0 0 u G0 G1",
+          "g 0 1 u G0 G1", "g 0 1 l G0 G1", "q 0 0", "pick 0 0 52",
+          "g 1 0 u G0 G1", "g 1 0 l G0 G1",
+          "g 1 1 u G0 G1", "g 1 1 l G0 G1", "q 1 1", "pick 1 0 32", "zeros",
+          "x 0 X1", "x 1 X1", "q 0 1", "q 1 0",
+          "g 2 0 u G0 G1", "g 2 0 l^ G0 G1",
+          "g 2 1 u G0 G1", "g 2 1 l^ G0 G1", "q 2 0", "x 2 X0", "q 2 1", "q 3 0",
+          "g 3 0 u G0", "g 3 0 l^ G0", "g 3 0 u G1",
+          "g 3 1 u G0", "g 3 1 l^ G0", "q 3 1", "g 3 1 u G1", "q 3 2"]
+SCALAR = ["turn 10 12", "fill 10 12", "turn 12 16", "fill 12 16", "g 0 0 l G0 G1", "zc 4 6 q0_0",
+          "pick 0 52 128", "drop 0 8 16", "pick 1 32 128", "drop 1 8 16",
+          "g 2 0 l_ G0 G1", "g 2 1 l_ G0 G1", "x 2 X1", "x 3 X0", "x 3 X1",
+          "g 3 0 l_ G0", "g 3 0 l G1", "g 3 1 l_ G0", "g 3 1 l G1"]
+SYNC = ["spread", "fill 0 2", "fill 2 6", "fill 6 10", "drop 0 0 8", "drop 1 0 8"]
+PRODUCTS = "000 001 010 011 100 101 110 111 200 201 300 310 301 311 210 211".split()
 COPIES = {"S": ["00", "01"], "V": ["10", "11"]}
 STORES = {"sync": ["00", "10", "11"], "scalar": ["01"]}
 
 CALLS = {
-    "c0": ("rank", ["q0_0"], [("c", 0, 256, "near", (8, 16, 4)), ("c", 256, 512, "far", (10, 16, 4))]),
-    "c1": ("rank", ["q1_0"], [("c", 512, 768, "home", (0, 8, 2)), ("c", 768, 1024, "far", (8, 16, 2)), ("p", 0, 1024, "near", (1, 8, 2))]),
+    "c0": ("rank", ["q0_0"], [("c", 0, 256, "near", (0, 8, 1))]),
+    "b1": ("rank", ["q1_1"], [("c", 768, 1024, "near", (0, 8, 1))]),
+    "c1": ("rank", ["q0_1", "q1_0"], [("c", 512, 768, "home", (0, 8, 2)), ("c", 256, 512, "far", (8, 16, 2)),
+                                      ("p", 0, 1024, "near", (1, 8, 2))]),
     "x2": ("rank", ["q2_0"], [("c", 1024, 1152, "home", (0, 8, 1)), ("c", 1152, 1280, "far", (8, 16, 2))]),
     "g2": ("rank", ["q2_1"], [("c", 1280, 1408, "home", (0, 8, 2)), ("p", 1024, 1536, "home", (1, 8, 2))]),
     "k2": ("rank", ["q2_1"], [("c", 1408, 1536, "home", (0, 8, 1))]),
-    "n0": ("near", ["hc0"], [("c", 0, 256, "door", (0, 8, 1))]),
-    "f0": ("far", ["hc0"], [("c", 256, 512, "home", (0, 8, 1))]),
-    "f1": ("far", ["hc1"], [("c", 768, 1024, "home", (0, 8, 1))]),
+    "n0": ("near", ["hc0"], [("c", 0, 128, "door", (0, 8, 1)), ("c", 128, 256, "far", (8, 16, 1))]),
+    "nb": ("near", ["hb1"], [("c", 768, 896, "door", (0, 8, 1)), ("c", 896, 1024, "far", (8, 16, 1))]),
+    "f0": ("far", ["hn0"], [("c", 128, 256, "home", (0, 8, 1))]),
+    "fb": ("far", ["hnb"], [("c", 896, 1024, "home", (0, 8, 1))]),
+    "f1": ("far", ["hc1"], [("c", 256, 512, "home", (0, 8, 1))]),
     "n1": ("near", ["hc1"], [("p", 0, 512, "home", (0, 4, 1)), ("p", 512, 1024, "home", (4, 8, 1))]),
     "f2": ("far", ["hx2"], [("c", 1152, 1280, "home", (0, 8, 1))]),
-    "d0": ("door", ["hn0"], [("c", 0, 256, "home", (0, 8, 1))]),
+    "d0": ("door", ["hn0"], [("c", 0, 128, "home", (0, 8, 1))]),
+    "db": ("door", ["hnb"], [("c", 768, 896, "home", (0, 8, 1))]),
 }
 
 SCRATCH = {
     "idx": ("sbuf", [128, 16], "int32"),
-    "tab": ("dram", [ROWS, RW], "bfloat16"),
+    "ix": ("sbuf", [128, N, 4], "int32"),
     "ps": ("psum", [128, 2048], "float32"),
     "yo": ("sbuf", [128, GW], "float32"),
     "cq": ("sbuf", [128, N * C], "float8_e4m3fn_x4"),
     "sq": ("sbuf", [128, N * C], "uint8"),
     "cin": ("sbuf", [128, (N - 1) * C], "float8_e4m3fn_x4"),
     "sin": ("sbuf", [128, (N - 1) * C], "uint8"),
-    "land": ("sbuf", [128, 2 * N * RW], "bfloat16"),
+    "land": ("sbuf", [128, 2 * N * GW], "bfloat16"),
+    "zb": ("sbuf", [128, 2 * GW], "bfloat16"),
+    "xs": ("sbuf", [128, ROWS // XP, XW], "bfloat16"),
+    "xr": ("sbuf", [128, GRP, ROWS // XP, F], "bfloat16"),
+    "win": ("sbuf", [128, F + ROWS * F], "bfloat16"),
+    "got": ("sbuf", [128, 2 * PK], "bfloat16"),
+    "stage": ("sbuf", [128, GRP, 2, 4 * F], "bfloat16"),
+    "oa": ("sbuf", [128, N, 32], "float32"),
+    "ob": ("sbuf", [128, N, 32], "float32"),
+    "off": ("sbuf", [128, 2 * PK // GRP], "uint16"),
 }
 for _k in range(N):
-    SCRATCH["tile%d" % _k] = ("sbuf", [128, 4 * C], "bfloat16")
+    SCRATCH["gt%d" % _k] = ("sbuf", [128, 8 * W], "bfloat16")
+SCRATCH["xt"] = ("sbuf", [128, 2, 8 * W], "bfloat16")
 
-SEMAPHORES = ["idx", "tab", "tabx", "sent", "stsync", "stscalar"]
+SEMAPHORES = ["idx", "ix", "z1", "z2", "zd", "sent", "stsync", "stscalar", "xs", "oa", "ob", "win", "got0", "got1", "xl0", "xl1"]
+SEMAPHORES += ["tn" + _w.split()[1] for _w in VECTOR + SCALAR if _w.startswith("turn")]
 for _q in ("00", "01", "10", "11"):
     SEMAPHORES += ["mm" + _q, "yc" + _q]
 for _k in range(N):
-    SEMAPHORES += ["zt%d" % _k, "ga%d_0" % _k, "ga%d_1" % _k]
-    for _j in range(4):
+    SEMAPHORES += ["ga%d_0" % _k, "ga%d_1" % _k]
+    for _j in range(len(TILES[_k].split("|"))):
         SEMAPHORES += ["cp%d_%d" % (_k, _j), "q%d_%d" % (_k, _j)]
 for _s in CALLS:
     SEMAPHORES += ["h" + _s] + sorted(set("a%s_%d" % (_s, _t[1] // C) for _t in CALLS[_s][2] if _t[3] == "home"))
@@ -105,12 +133,16 @@ def rank_program(g, core, T, topo):
             return T["cin" if home else "cq"][:, lo:hi].bitcast(dt.uint8)
         return T["sin" if home else "sq"][:, lo:hi]
 
+    work = [w.split() for w in VECTOR + SCALAR]
+    fills = lambda sem: sum(1 for w in work if w[0] in ("z", "zc") and w[3] == sem)
     waited = []
 
-    def wait(q, sem):
+    def wait(q, sem, count=None):
         if (q, sem) not in waited:
             waited.append((q, sem))
-            (g.tensor if q == "tensor" else g).wait_ge(S[sem], 1 if sem[0] == "q" else 16 if sem[0] == "g" else landing(core, sem))
+            if count is None:
+                count = 1 + fills(sem) if sem[0] == "q" else landing(core, sem)
+            {"g": g, "tensor": g.tensor, "vector": g.vector, "scalar": g.scalar, "sync": g.sync}[q].wait_ge(S[sem], count)
 
     def issue(a, name):
         for sem in CALLS[name][1]:
@@ -138,71 +170,115 @@ def rank_program(g, core, T, topo):
 
     g.sync.dma_start(T.idx[0:64, :], T.pick[0:64, :]).then_inc(S["idx"], 16)
     g.scalar.dma_start(T.idx[64:128, 0:14], T.pick[0:64, 2:16]).then_inc(S["idx"], 16)
-    g.sync.dma_start(T.tab[:, XW:RW], T.dy[:]).then_inc(S["tab"], 16)
-    g.scalar.dma_start(T.tab[GX:ROWS, 0:XW], T.x[GX:ROWS, :]).then_inc(S["tab"], 16)
-    g.dma_start(T.tab[0:GX, 0:XW], T.x[0:GX, :]).then_inc(S["tabx"], 16)
-    g.sync.wait_ge(S["tabx"], 16)
-    g.sync.sem_inc(S["tab"], 1)
-
-    column = lambda k, part: W * TILES[k][0].split().index(part)
-    g.vector.memset(T.land[:, 0:RW], 0.0).then_inc(S["idx"], 1)
-    g.vector.memset(T.land[:, RW:2 * N * RW], 0.0).then_inc(S["tab"], 1)
-    for k in range(N):
-        for h, part in (("l", "X0"), ("u", "X1")):
-            c = column(k, part)
-            g.vector.memset(T["tile%d" % k][half[h], 4 * c:4 * (c + W)], 0.0).then_inc(S["zt%d" % k], 1)
-
-    def gather(k, i, table):
-        col = 4 * lists[k] + i
-        off = IndirectOffsetOnAxis(ap=T.idx[:, col:col + 1], axis=0)
-        sem = S["ga%d_%d" % (k, i)]
-        o = RW * (2 * k + i)
-        for lo, hi, src in [(0, RW, T.tab)] if table else [(XW, RW, T.dy), (0, XW, T.x)]:
-            g.indirect_dma_start(T.land[:, o + lo:o + hi], None, src[:], off, bounds_check=ROWS - 1, oob_is_err=False).then_inc(sem, 16)
+    g.sync.dma_start(T.xs[0:XP // 2], T.x[0:ROWS // 2, :]).then_inc(S["xs"], 16)
+    g.scalar.dma_start(T.xs[XP // 2:XP], T.x[ROWS // 2:ROWS, :]).then_inc(S["xs"], 16)
+    g.dma_start(T.ix[0:64], T.pick[0:64, :]).then_inc(S["ix"], 16)
 
     sent = 0
-    g.wait_ge(S["idx"], 33)
+    g.wait_ge(S["idx"], 32 + fills("idx"))
     for step in PLAN:
-        if step == "tab":
-            g.wait_ge(S["tab"], 34)
-        elif step in CALLS:
+        if step in CALLS:
             sent += issue(r, step)
+        elif step[0] == "z":
+            g.wait_ge(S[step], 80 if step == "zd" else 1)
         else:
-            gather(int(step[1]), int(step[2]), step[0] == "t")
+            k, i = int(step[1]), int(step[2])
+            col, o = 4 * lists[k] + i, GW * (2 * k + i)
+            g.indirect_dma_start(T.land[:, o:o + GW], None, T.dy[:], IndirectOffsetOnAxis(ap=T.idx[:, col:col + 1], axis=0),
+                                 bounds_check=ROWS - 1, oob_is_err=False).then_inc(S["ga%d_%d" % (k, i)], 16)
     g.wait_ge(S["sent"], sent)
 
-    group = {}
-    for k in range(N):
-        tile = T["tile%d" % k]
-        calls = [w.split()[1:] for w in TILES[k][1] if w[0] == "q"]
-        for j, parts in enumerate(calls):
-            for part in parts:
-                group[k, part] = j
-        first = lambda parts: min(group[k, part] for part in parts)
-        sources = lambda op: [("u", 0), ("l", 2)][op[1:] == "_":2 - (op[1:] == "^")]
-        copies = [w.split() for w in TILES[k][1] + TILES[k][2] if w[0] != "q"]
-        count = [2 * sum(len(sources(w[0])) for w in copies if first(w[1:]) == j) for j in range(len(calls))]
-        for i in range(2):
-            o = RW * (2 * k + i)
-            for q, work in ((g.vector, TILES[k][1]), (g.scalar, TILES[k][2])):
-                q.wait_ge(S["ga%d_%d" % (k, i)], 32 if "d%d%d" % (k, i) in PLAN else 16)
-                for op, *parts in [w.split() for w in work]:
-                    lo, n = column(k, parts[0]), W * len(parts)
-                    if op != "q":
-                        for p, t in sources(op):
-                            a = tile[half[op[0]], 4 * lo + i + t:4 * (lo + n):4]
-                            s = o + SOURCE[op[0]][parts[0]]
-                            b = T.land[half[p], s:s + n]
-                            call = q.tensor_copy(a, b) if work is TILES[k][1] else q.activation(a, b, ActivationFunctionType.Copy)
-                            call.then_inc(S["cp%d_%d" % (k, first(parts))], 1)
-                    elif i == 1:
-                        j = first(parts)
-                        if j == 0:
-                            q.wait_ge(S["zt%d" % k], 2)
-                        if count[j]:
-                            q.wait_ge(S["cp%d_%d" % (k, j)], count[j])
-                        c = slice(C * k + lo, C * k + lo + n)
-                        q.quantize_mx(T.cq[:, c], T.sq[:, c], tile[:, 4 * lo:4 * (lo + n)]).then_inc(S["q%d_%d" % (k, j)], 1)
+    column = lambda k, part: W * TILES[k].replace("|", " ").split().index(part)
+    group = lambda k, part: [part in c for c in TILES[k].split("|")].index(True)
+    sources = lambda op: [("u", 0), ("l", 2)][op[1:] == "_":2 - (op[1:] == "^")]
+
+    def copies(k, j):
+        n = 0
+        for w in work:
+            if w[0] == "g" and int(w[1]) == k and group(k, w[4]) == j:
+                n += len(sources(w[3]))
+            if w[0] == "x" and int(w[1]) == k and group(k, w[2]) == j:
+                n += 1
+        return n
+
+    tile = lambda k, part, rows, cols: T.xt[rows, k % 2, cols] if part[0] == "X" else T["gt%d" % k][rows, cols]
+    at = lambda part: 4 * W * int(part[1])
+
+    picks = lambda rd: sum(1 for w in work if w[0] == "pick" and int(w[1]) == rd)
+    for name, q, script in (("vector", g.vector, VECTOR), ("scalar", g.scalar, SCALAR), ("sync", g.sync, SYNC)):
+        move = lambda a, b: q.tensor_copy(a, b) if name == "vector" else q.activation(a, b, ActivationFunctionType.Copy)
+        for op, *w in [s.split() for s in script]:
+            n = [int(v) for v in w if v.isdigit()]
+            if op == "z":
+                q.memset(T.land[:, GW * n[0]:GW * n[1]], 0.0).then_inc(S[w[2]], 1)
+            elif op == "small":
+                q.memset(T.win[:, 0:F], 0.0).then_inc(S["win"], 1)
+                q.memset(T.off[64:128, :], 0).then_inc(S["win"], 1)
+                q.memset(T.oa[0:64, :, GRP:32], 0.0).then_inc(S["oa"], 1)
+            elif op == "zb":
+                q.memset(T.zb[:, :], 0.0).then_inc(S["z2"], 1)
+            elif op == "spread":
+                wait(name, "z2", 1)
+                q.dma_start(T.land[:, 6 * GW:8 * GW], T.zb[:, :]).then_inc(S["zd"], 16)
+                for h, part in (("l", "X0"), ("u", "X1")):
+                    q.dma_start(T.xt[half[h], :, at(part):at(part) + 4 * W], T.zb[half[h], :]).then_inc(S["zd"], 16)
+            elif op == "zc":
+                wait(name, "z2", 1)
+                move(T.land[:, GW * n[0]:GW * n[1]], T.zb[:, :]).then_inc(S[w[2]], 1)
+            elif op == "zeros":
+                wait(name, "zd", 48)
+            elif op == "turn":
+                wait(name, "xs", 32)
+                for c in range(*n):
+                    move(T.xr[0:XP, c, :, :], T.xs[0:XP, :, F * c:F * c + F]).then_inc(S["tn" + w[0]], 1)
+            elif op == "fill":
+                wait(name, "tn" + w[0], n[1] - n[0])
+                for c in range(*n):
+                    for p in range(c, 64, 32):
+                        q.dma_start(T.win[p:p + 1, F:], T.xr[0:XP, c, :, :]).then_inc(S["win"], 16)
+            elif op == "offsets":
+                wait(name, "ix", 16)
+                for j in range(4):
+                    q.tensor_scalar(T.oa[0:64, :, 4 * j:4 * j + 4], T.ix[0:64], float(F), float(F + j),
+                                    AluOpType.mult, AluOpType.add).then_inc(S["oa"], 1)
+                wait(name, "oa", 5)
+                q.transpose(T.ob[0:64], T.oa[0:64]).then_inc(S["ob"], 1)
+                wait(name, "ob", 1)
+                for k in range(N):
+                    for h in range(2):
+                        o = 128 * (k // 2)
+                        q.tensor_scalar(T.off[0:64, o + 2 * (k % 2) + h:o + 128:4], T.ob[0:64, lists[k], :], float(4 * h), None,
+                                        AluOpType.add).then_inc(S["win"], 1)
+            elif op == "pick":
+                wait(name, "win", 16 * R * GRP + 2 + 2 * N)
+                lo, hi = 128 * n[0] + n[1], 128 * n[0] + n[2]
+                move(T.got[:, GRP * lo:GRP * hi], T.win[:, :].indirect(T.off[:, lo:hi])).then_inc(S["got" + w[0]], 1)
+            elif op == "drop":
+                wait(name, "got" + w[0], picks(n[0]))
+                for c in range(n[1], n[2]):
+                    q.dma_start(T.stage[0:64, c, :, :] if n[0] else T.xt[0:64, :, 4 * F * c:4 * F * (c + 1)], T.got[c:64:32, PK * n[0]:PK * n[0] + PK]).then_inc(S["xl" + w[0]], 16)
+            elif op == "x":
+                k, part = n[0], w[1]
+                wait(name, "xl%d" % (k // 2), 16 * GRP)
+                if k >= 2:
+                    wait(name, "q%d_%d" % (k - 2, group(k - 2, part)))
+                move(tile(k, part, half["u" if part == "X0" else "l"], slice(at(part), at(part) + 4 * W)),
+                     T.stage[0:64, :, k % 2, :] if k >= 2 else T.xt[0:64, k, 0:4 * W]).then_inc(S["cp%d_%d" % (k, group(k, part))], 1)
+            elif op == "g":
+                k, i = n
+                wait(name, "ga%d_%d" % (k, i), 16)
+                lo, wide = at(w[3]), W * len(w[3:])
+                for p, t in sources(w[2]):
+                    s = GW * (2 * k + i) + SOURCE[w[2][0]][w[3]]
+                    move(tile(k, "G", half[w[2][0]], slice(lo + i + t, lo + 4 * wide, 4)),
+                         T.land[half[p], s:s + wide]).then_inc(S["cp%d_%d" % (k, group(k, w[3]))], 1)
+            elif op == "q":
+                k, j = n
+                parts = TILES[k].split("|")[j].split()
+                wait(name, "cp%d_%d" % (k, j), copies(k, j))
+                lo, wide = column(k, parts[0]), W * len(parts)
+                c = slice(C * k + lo, C * k + lo + wide)
+                q.quantize_mx(T.cq[:, c], T.sq[:, c], tile(k, parts[0], slice(0, 128), slice(at(parts[0]), at(parts[0]) + 4 * wide))).then_inc(S["q%d_%d" % (k, j)], 1)
 
     bank = lambda q: T.ps[:, 512 * int(q, 2):512 * int(q, 2) + W]
     for j, step in enumerate(PRODUCTS):
@@ -211,7 +287,7 @@ def rank_program(g, core, T, topo):
         for part in ("X" + q[0], "G" + q[1]):
             lo = C * k + column(k, part)
             if k == N - 1:
-                wait("tensor", "q%d_%d" % (k, group[k, part]))
+                wait("tensor", "q%d_%d" % (k, group(k, part)))
             else:
                 for a in range(N):
                     for name in CALLS:

from concourse.bass import DstId, RemoteDMATransfer, IndirectOffsetOnAxis
from concourse.mybir import dt, ActivationFunctionType, AluOpType

N = 4
ALL = 112
ROWS = 1024
XW, GW = 128, 512
C = 512
W = 128
GRP = 16
F = XW // GRP
XP = 64
R = 2
PK = 2 * 256 * F // R

PLAN = "d00 d01 z1 d10 d11 c0 d20 b1 d21 c1 d30 x2 d31 g2 k2".split()

TILES = ["G0 G1|X0 X1", "X0 X1|G0 G1", "G0 G1|X0 X1", "X0 X1|G0|G1"]
SOURCE = {"u": {"G0": 0, "G1": W}, "l": {"G0": 2 * W, "G1": 3 * W}}
VECTOR = ["z 0 2 idx", "zb", "z 2 4 z1", "small", "turn 0 2", "turn 2 6", "turn 6 10", "offsets",
          "g 0 0 u G0 G1",
          "g 0 1 u G0 G1", "g 0 1 l G0 G1", "q 0 0", "pick 0 0 52",
          "g 1 0 u G0 G1", "g 1 0 l G0 G1",
          "g 1 1 u G0 G1", "g 1 1 l G0 G1", "q 1 1", "pick 1 0 32", "zeros",
          "x 0 X1", "x 1 X1", "q 0 1", "q 1 0",
          "g 2 0 u G0 G1", "g 2 0 l^ G0 G1",
          "g 2 1 u G0 G1", "g 2 1 l^ G0 G1", "q 2 0", "x 2 X0", "q 2 1", "q 3 0",
          "g 3 0 u G0", "g 3 0 l^ G0", "g 3 0 u G1",
          "g 3 1 u G0", "g 3 1 l^ G0", "q 3 1", "g 3 1 u G1", "q 3 2"]
SCALAR = ["turn 10 12", "fill 10 12", "turn 12 16", "fill 12 16", "g 0 0 l G0 G1", "zc 4 6 q0_0",
          "pick 0 52 128", "drop 0 8 16", "pick 1 32 128", "drop 1 8 16",
          "g 2 0 l_ G0 G1", "g 2 1 l_ G0 G1", "x 2 X1", "x 3 X0", "x 3 X1",
          "g 3 0 l_ G0", "g 3 0 l G1", "g 3 1 l_ G0", "g 3 1 l G1"]
SYNC = ["spread", "fill 0 2", "fill 2 6", "fill 6 10", "drop 0 0 8", "drop 1 0 8"]
PRODUCTS = "000 001 010 011 100 101 110 111 200 201 300 310 301 311 210 211".split()
COPIES = {"S": ["00", "01"], "V": ["10", "11"]}
STORES = {"sync": ["00", "10", "11"], "scalar": ["01"]}

CALLS = {
    "c0": ("rank", ["q0_0"], [("c", 0, 256, "near", (0, 8, 1))]),
    "b1": ("rank", ["q1_1"], [("c", 768, 1024, "near", (0, 8, 1))]),
    "c1": ("rank", ["q0_1", "q1_0"], [("c", 512, 768, "home", (0, 8, 2)), ("c", 256, 512, "far", (8, 16, 2)),
                                      ("p", 0, 1024, "near", (1, 8, 2))]),
    "x2": ("rank", ["q2_0"], [("c", 1024, 1152, "home", (0, 8, 1)), ("c", 1152, 1280, "far", (8, 16, 2))]),
    "g2": ("rank", ["q2_1"], [("c", 1280, 1408, "home", (0, 8, 2)), ("p", 1024, 1536, "home", (1, 8, 2))]),
    "k2": ("rank", ["q2_1"], [("c", 1408, 1536, "home", (0, 8, 1))]),
    "n0": ("near", ["hc0"], [("c", 0, 128, "door", (0, 8, 1)), ("c", 128, 256, "far", (8, 16, 1))]),
    "nb": ("near", ["hb1"], [("c", 768, 896, "door", (0, 8, 1)), ("c", 896, 1024, "far", (8, 16, 1))]),
    "f0": ("far", ["hn0"], [("c", 128, 256, "home", (0, 8, 1))]),
    "fb": ("far", ["hnb"], [("c", 896, 1024, "home", (0, 8, 1))]),
    "f1": ("far", ["hc1"], [("c", 256, 512, "home", (0, 8, 1))]),
    "n1": ("near", ["hc1"], [("p", 0, 512, "home", (0, 4, 1)), ("p", 512, 1024, "home", (4, 8, 1))]),
    "f2": ("far", ["hx2"], [("c", 1152, 1280, "home", (0, 8, 1))]),
    "d0": ("door", ["hn0"], [("c", 0, 128, "home", (0, 8, 1))]),
    "db": ("door", ["hnb"], [("c", 768, 896, "home", (0, 8, 1))]),
}

SCRATCH = {
    "idx": ("sbuf", [128, 16], "int32"),
    "ix": ("sbuf", [128, N, 4], "int32"),
    "ps": ("psum", [128, 2048], "float32"),
    "yo": ("sbuf", [128, GW], "float32"),
    "cq": ("sbuf", [128, N * C], "float8_e4m3fn_x4"),
    "sq": ("sbuf", [128, N * C], "uint8"),
    "cin": ("sbuf", [128, (N - 1) * C], "float8_e4m3fn_x4"),
    "sin": ("sbuf", [128, (N - 1) * C], "uint8"),
    "land": ("sbuf", [128, 2 * N * GW], "bfloat16"),
    "zb": ("sbuf", [128, 2 * GW], "bfloat16"),
    "xs": ("sbuf", [128, ROWS // XP, XW], "bfloat16"),
    "xr": ("sbuf", [128, GRP, ROWS // XP, F], "bfloat16"),
    "win": ("sbuf", [128, F + ROWS * F], "bfloat16"),
    "got": ("sbuf", [128, 2 * PK], "bfloat16"),
    "stage": ("sbuf", [128, GRP, 2, 4 * F], "bfloat16"),
    "oa": ("sbuf", [128, N, 32], "float32"),
    "ob": ("sbuf", [128, N, 32], "float32"),
    "off": ("sbuf", [128, 2 * PK // GRP], "uint16"),
}
for _k in range(N):
    SCRATCH["gt%d" % _k] = ("sbuf", [128, 8 * W], "bfloat16")
SCRATCH["xt"] = ("sbuf", [128, 2, 8 * W], "bfloat16")

SEMAPHORES = ["idx", "ix", "z1", "z2", "zd", "sent", "stsync", "stscalar", "xs", "oa", "ob", "win", "got0", "got1", "xl0", "xl1"]
SEMAPHORES += ["tn" + _w.split()[1] for _w in VECTOR + SCALAR if _w.startswith("turn")]
for _q in ("00", "01", "10", "11"):
    SEMAPHORES += ["mm" + _q, "yc" + _q]
for _k in range(N):
    SEMAPHORES += ["ga%d_0" % _k, "ga%d_1" % _k]
    for _j in range(len(TILES[_k].split("|"))):
        SEMAPHORES += ["cp%d_%d" % (_k, _j), "q%d_%d" % (_k, _j)]
for _s in CALLS:
    SEMAPHORES += ["h" + _s] + sorted(set("a%s_%d" % (_s, _t[1] // C) for _t in CALLS[_s][2] if _t[3] == "home"))


def rank_program(g, core, T, topo):
    cores = T.cores
    S = T.sem
    plane = lambda m: sum(1 for a in range(N) if topo.same_plane(topo.chip(cores[a]), topo.chip(cores[a ^ m])))
    order = sorted(range(1, N), key=lambda m: (plane(m), m))

    def team(a):
        c = cores[a]
        free = [h for h in topo.cores_of(c) if h != c and all(topo.may_write(h, d) for d in cores)]
        doors = [h for h in range(ALL) if topo.mates(topo.chip(h), topo.chip(c)) and topo.may_write(h, c)]
        far = [h for h in free if topo.die(h) != topo.die(c)]
        return {"rank": c, "far": far[0], "far2": far[1],
                "near": [h for h in free if topo.die(h) == topo.die(c)][0],
                "door": [h for h in doors if topo.die(h) == topo.die(c)][0],
                "door2": [h for h in doors if topo.die(h) != topo.die(c)][0]}

    teams = [team(a) for a in range(N)]

    def role(a, who, col):
        home = a ^ order[col // C]
        if who == "home":
            return cores[home]
        return teams[home if who.startswith("door") else a][who]

    issuer = lambda a, name: role(a, CALLS[name][0], CALLS[name][2][0][1])

    def transfers(a, name):
        src, out = issuer(a, name), []
        for kind, lo, hi, to, share in CALLS[name][2]:
            dst = role(a, to, lo)
            out.append((kind, lo, hi, dst, "a%s_%d" % (name, lo // C) if to == "home" else "h" + name,
                        topo.engines(src, dst)[slice(*share)]))
        return out

    def landing(dst, sem):
        return sum(len(t[5]) for a in range(N) for name in CALLS for t in transfers(a, name) if t[3] == dst and t[4] == sem)

    def view(kind, lo, hi, home):
        if kind == "c":
            return T["cin" if home else "cq"][:, lo:hi].bitcast(dt.uint8)
        return T["sin" if home else "sq"][:, lo:hi]

    work = [w.split() for w in VECTOR + SCALAR]
    fills = lambda sem: sum(1 for w in work if w[0] in ("z", "zc") and w[3] == sem)
    waited = []

    def wait(q, sem, count=None):
        if (q, sem) not in waited:
            waited.append((q, sem))
            if count is None:
                count = 1 + fills(sem) if sem[0] == "q" else landing(core, sem)
            {"g": g, "tensor": g.tensor, "vector": g.vector, "scalar": g.scalar, "sync": g.sync}[q].wait_ge(S[sem], count)

    def issue(a, name):
        for sem in CALLS[name][1]:
            wait("g", sem)
        trs = []
        for kind, lo, hi, dst, sem, es in transfers(a, name):
            rid, pid, _ = topo.addr(dst)
            trs.append((view(kind, lo, hi, dst in cores), view(kind, lo, hi, False), S[sem], pid, rid, sum(1 << e for e in es)))
        if len(trs) == 1:
            dst, src, sem, pid, rid, mask = trs[0]
            g.remote_dma(dst, src, sem, S["sent"], pid, rid, mask)
        else:
            g.remote_dma_fused([RemoteDMATransfer(dst_ids=[DstId(rid=rid, pnc=pid)], dma_engine_mask=mask, remote_sem=sem,
                                                  src=src, dst=dst) for dst, src, sem, pid, rid, mask in trs], local_sem=S["sent"])
        return sum(len(t[5]) for t in transfers(a, name))

    r = T.rank_of(core)
    if r is None:
        sent = sum([issue(a, name) for name in CALLS for a in range(N) if issuer(a, name) == core])
        if sent:
            g.wait_ge(S["sent"], sent)
        return
    lists = [r ^ m for m in order] + [r]
    half = {"u": slice(0, 64), "l": slice(64, 128)}

    g.sync.dma_start(T.idx[0:64, :], T.pick[0:64, :]).then_inc(S["idx"], 16)
    g.scalar.dma_start(T.idx[64:128, 0:14], T.pick[0:64, 2:16]).then_inc(S["idx"], 16)
    g.sync.dma_start(T.xs[0:XP // 2], T.x[0:ROWS // 2, :]).then_inc(S["xs"], 16)
    g.scalar.dma_start(T.xs[XP // 2:XP], T.x[ROWS // 2:ROWS, :]).then_inc(S["xs"], 16)
    g.dma_start(T.ix[0:64], T.pick[0:64, :]).then_inc(S["ix"], 16)

    sent = 0
    g.wait_ge(S["idx"], 32 + fills("idx"))
    for step in PLAN:
        if step in CALLS:
            sent += issue(r, step)
        elif step[0] == "z":
            g.wait_ge(S[step], 80 if step == "zd" else 1)
        else:
            k, i = int(step[1]), int(step[2])
            col, o = 4 * lists[k] + i, GW * (2 * k + i)
            g.indirect_dma_start(T.land[:, o:o + GW], None, T.dy[:], IndirectOffsetOnAxis(ap=T.idx[:, col:col + 1], axis=0),
                                 bounds_check=ROWS - 1, oob_is_err=False).then_inc(S["ga%d_%d" % (k, i)], 16)
    g.wait_ge(S["sent"], sent)

    column = lambda k, part: W * TILES[k].replace("|", " ").split().index(part)
    group = lambda k, part: [part in c for c in TILES[k].split("|")].index(True)
    sources = lambda op: [("u", 0), ("l", 2)][op[1:] == "_":2 - (op[1:] == "^")]

    def copies(k, j):
        n = 0
        for w in work:
            if w[0] == "g" and int(w[1]) == k and group(k, w[4]) == j:
                n += len(sources(w[3]))
            if w[0] == "x" and int(w[1]) == k and group(k, w[2]) == j:
                n += 1
        return n

    tile = lambda k, part, rows, cols: T.xt[rows, k % 2, cols] if part[0] == "X" else T["gt%d" % k][rows, cols]
    at = lambda part: 4 * W * int(part[1])

    picks = lambda rd: sum(1 for w in work if w[0] == "pick" and int(w[1]) == rd)
    for name, q, script in (("vector", g.vector, VECTOR), ("scalar", g.scalar, SCALAR), ("sync", g.sync, SYNC)):
        move = lambda a, b: q.tensor_copy(a, b) if name == "vector" else q.activation(a, b, ActivationFunctionType.Copy)
        for op, *w in [s.split() for s in script]:
            n = [int(v) for v in w if v.isdigit()]
            if op == "z":
                q.memset(T.land[:, GW * n[0]:GW * n[1]], 0.0).then_inc(S[w[2]], 1)
            elif op == "small":
                q.memset(T.win[:, 0:F], 0.0).then_inc(S["win"], 1)
                q.memset(T.off[64:128, :], 0).then_inc(S["win"], 1)
                q.memset(T.oa[0:64, :, GRP:32], 0.0).then_inc(S["oa"], 1)
            elif op == "zb":
                q.memset(T.zb[:, :], 0.0).then_inc(S["z2"], 1)
            elif op == "spread":
                wait(name, "z2", 1)
                q.dma_start(T.land[:, 6 * GW:8 * GW], T.zb[:, :]).then_inc(S["zd"], 16)
                for h, part in (("l", "X0"), ("u", "X1")):
                    q.dma_start(T.xt[half[h], :, at(part):at(part) + 4 * W], T.zb[half[h], :]).then_inc(S["zd"], 16)
            elif op == "zc":
                wait(name, "z2", 1)
                move(T.land[:, GW * n[0]:GW * n[1]], T.zb[:, :]).then_inc(S[w[2]], 1)
            elif op == "zeros":
                wait(name, "zd", 48)
            elif op == "turn":
                wait(name, "xs", 32)
                for c in range(*n):
                    move(T.xr[0:XP, c, :, :], T.xs[0:XP, :, F * c:F * c + F]).then_inc(S["tn" + w[0]], 1)
            elif op == "fill":
                wait(name, "tn" + w[0], n[1] - n[0])
                for c in range(*n):
                    for p in range(c, 64, 32):
                        q.dma_start(T.win[p:p + 1, F:], T.xr[0:XP, c, :, :]).then_inc(S["win"], 16)
            elif op == "offsets":
                wait(name, "ix", 16)
                for j in range(4):
                    q.tensor_scalar(T.oa[0:64, :, 4 * j:4 * j + 4], T.ix[0:64], float(F), float(F + j),
                                    AluOpType.mult, AluOpType.add).then_inc(S["oa"], 1)
                wait(name, "oa", 5)
                q.transpose(T.ob[0:64], T.oa[0:64]).then_inc(S["ob"], 1)
                wait(name, "ob", 1)
                for k in range(N):
                    for h in range(2):
                        o = 128 * (k // 2)
                        q.tensor_scalar(T.off[0:64, o + 2 * (k % 2) + h:o + 128:4], T.ob[0:64, lists[k], :], float(4 * h), None,
                                        AluOpType.add).then_inc(S["win"], 1)
            elif op == "pick":
                wait(name, "win", 16 * R * GRP + 2 + 2 * N)
                lo, hi = 128 * n[0] + n[1], 128 * n[0] + n[2]
                move(T.got[:, GRP * lo:GRP * hi], T.win[:, :].indirect(T.off[:, lo:hi])).then_inc(S["got" + w[0]], 1)
            elif op == "drop":
                wait(name, "got" + w[0], picks(n[0]))
                for c in range(n[1], n[2]):
                    q.dma_start(T.stage[0:64, c, :, :] if n[0] else T.xt[0:64, :, 4 * F * c:4 * F * (c + 1)], T.got[c:64:32, PK * n[0]:PK * n[0] + PK]).then_inc(S["xl" + w[0]], 16)
            elif op == "x":
                k, part = n[0], w[1]
                wait(name, "xl%d" % (k // 2), 16 * GRP)
                if k >= 2:
                    wait(name, "q%d_%d" % (k - 2, group(k - 2, part)))
                move(tile(k, part, half["u" if part == "X0" else "l"], slice(at(part), at(part) + 4 * W)),
                     T.stage[0:64, :, k % 2, :] if k >= 2 else T.xt[0:64, k, 0:4 * W]).then_inc(S["cp%d_%d" % (k, group(k, part))], 1)
            elif op == "g":
                k, i = n
                wait(name, "ga%d_%d" % (k, i), 16)
                lo, wide = at(w[3]), W * len(w[3:])
                for p, t in sources(w[2]):
                    s = GW * (2 * k + i) + SOURCE[w[2][0]][w[3]]
                    move(tile(k, "G", half[w[2][0]], slice(lo + i + t, lo + 4 * wide, 4)),
                         T.land[half[p], s:s + wide]).then_inc(S["cp%d_%d" % (k, group(k, w[3]))], 1)
            elif op == "q":
                k, j = n
                parts = TILES[k].split("|")[j].split()
                wait(name, "cp%d_%d" % (k, j), copies(k, j))
                lo, wide = column(k, parts[0]), W * len(parts)
                c = slice(C * k + lo, C * k + lo + wide)
                q.quantize_mx(T.cq[:, c], T.sq[:, c], tile(k, parts[0], slice(0, 128), slice(at(parts[0]), at(parts[0]) + 4 * wide))).then_inc(S["q%d_%d" % (k, j)], 1)

    bank = lambda q: T.ps[:, 512 * int(q, 2):512 * int(q, 2) + W]
    for j, step in enumerate(PRODUCTS):
        k, q = int(step[0]), step[1:]
        sides = []
        for part in ("X" + q[0], "G" + q[1]):
            lo = C * k + column(k, part)
            if k == N - 1:
                wait("tensor", "q%d_%d" % (k, group(k, part)))
            else:
                for a in range(N):
                    for name in CALLS:
                        for t in transfers(a, name):
                            if t[3] == core and t[1] < lo + W and lo < t[2]:
                                wait("tensor", t[4])
            sides += [T["cq" if k == N - 1 else "cin"][:, lo:lo + W], T["sq" if k == N - 1 else "sin"][:, lo:lo + W]]
        mine = [s for s in PRODUCTS if s[1:] == q]
        op = g.tensor.matmul_mx(bank(q), *sides, step == mine[0], step == mine[-1])
        if step == mine[-1]:
            op.then_inc(S["mm" + q], 1)

    cols = lambda qs: slice(W * int(qs[0], 2), W * int(qs[-1], 2) + W)
    for q in COPIES["S"]:
        g.scalar.wait_ge(S["mm" + q], 1)
        g.scalar.activation(T.yo[:, cols([q])], bank(q), ActivationFunctionType.Copy).then_inc(S["yc" + q], 1)
    for q in COPIES["V"]:
        g.vector.wait_ge(S["mm" + q], 1)
        g.vector.tensor_copy(T.yo[:, cols([q])], bank(q)).then_inc(S["yc" + q], 1)
    for name, queue in (("sync", g.sync), ("scalar", g.scalar)):
        for qs in STORES[name]:
            for q in qs.split():
                queue.wait_ge(S["yc" + q], 1)
            queue.dma_start(T.y[:, cols(qs.split())], T.yo[:, cols(qs.split())]).then_inc(S["st" + name], 16)
        queue.wait_ge(S["st" + name], 16 * len(STORES[name]))
